import numpy as np
import ml_dtypes


def mxq(x, axis, fmt="e4m3"):
    dtype, down = {"e4m3": (ml_dtypes.float8_e4m3fn, 7), "e5m2": (ml_dtypes.float8_e5m2, 14)}[fmt]
    v = np.moveaxis(np.asarray(x, np.float32).astype(ml_dtypes.bfloat16).astype(np.float64), axis, -1)
    blocks = v.reshape(v.shape[:-1] + (-1, 32))
    amax = np.abs(blocks).max(-1, keepdims=True)
    byte = np.maximum(np.where(amax > 0, np.frexp(amax)[1] - 1 + 127, 0) - down, 1)
    scale = np.exp2(byte - 127.0)
    codes = (blocks / scale).astype(np.float32).astype(dtype).astype(np.float64)
    return np.moveaxis((codes * scale).reshape(v.shape), -1, axis)


WIDE = False


def mx_kscale(k):
    if not WIDE:
        return np.ones(k)
    levels = np.array([10, -10, 5, -5, 0])
    if k % 512:
        return np.exp2(np.random.permutation(np.resize(levels, k // 32))).repeat(32)
    a = np.empty((k // 512, 16))
    for p in range(k // 512):
        a[p, :8] = np.random.permutation(np.resize(levels, 8))
        for g in range(8):
            far = levels[np.abs(levels - a[p, g]) >= 10]
            a[p, g + 8] = far[np.random.randint(len(far))]
    return np.exp2(a.ravel()).repeat(32)


def f64(x):
    return np.asarray(x).astype(np.float64)


def striped(idx):
    return np.tile(idx.reshape(-1, 16).T, (8, 1)).astype(np.uint16)


def unstriped(offs):
    return offs[:16].T.reshape(-1).astype(np.int64)


def gelu(v):
    return 0.5 * v * (1.0 + np.tanh(np.sqrt(2.0 / np.pi) * (v + 0.044715 * v**3)))


K, T, S, N = 512, 1024, 512, 256


def setup_inputs():
    n = np.random.standard_normal
    s = mx_kscale(K)[:, None]
    w1, w2 = n((2, K, N)) / np.sqrt(2 * K) / s[None]
    return {
        "xT": (n((K, S)) * s).astype(np.float32),
        "sT": (n((K, T)) * s).astype(np.float32),
        "w1": w1.astype(np.float32),
        "w2": w2.astype(np.float32),
        "b": (0.3 * n((N, 1))).astype(np.float32),
        "offs": striped(np.random.permutation(T)[:S]),
    }


def reference(xT, sT, w1, w2, b, offs):
    y = mxq(f64(w1), 0, "e4m3").T @ mxq(f64(xT), 0, "e4m3") + mxq(f64(w2), 0, "e4m3").T @ mxq(f64(sT)[:, unstriped(offs)], 0, "e4m3")
    return gelu(y + f64(b))

@@ -1,0 +1,124 @@
+from contextlib import ExitStack
+
+import concourse.mybir as mybir
+
+K, T, S, N = 512, 1024, 512, 256
+
+F32 = mybir.dt.float32
+BF16 = mybir.dt.bfloat16
+U32 = mybir.dt.uint32
+U16 = mybir.dt.uint16
+U8 = mybir.dt.uint8
+FP8X4 = mybir.dt.float8_e4m3fn_x4
+GELU = mybir.ActivationFunctionType.Gelu_apprx_tanh
+
+P = 128
+M_TILES = N // P
+FLOPS = 2 * 2 * K * S * N
+
+X_LOADS = ((0, 384), (384, 512))
+GROUPS = ((0, 256), (256, 384), (384, 512))
+
+
+def tile_picked_recall_gelu_e_kernel(tc, xT, sT, w1, w2, b, offs, out):
+    nc = tc.nc
+    with ExitStack() as ctx:
+        keep = ctx.enter_context(tc.tile_pool(name="keep", bufs=1))
+        psum = ctx.enter_context(tc.psum_pool(name="psum", bufs=1))
+
+        offsets = keep.tile([P, S // 16], U16, name="offsets")
+        bias = keep.tile([P, M_TILES], F32, name="bias")
+        warm = keep.tile([P, 1], F32, name="warm")
+        raw_w = [keep.tile([P, 4, N], F32, name="raw_w%d" % i) for i in range(2)]
+        raw_s = [keep.tile([P, 2, T], F32, name="raw_s%d" % u) for u in range(2)]
+        raw_x = [keep.tile([P, 4, c1 - c0], F32, name="raw_x%d" % i) for i, (c0, c1) in enumerate(X_LOADS)]
+        pair_s = [keep.tile([P, T, 2], BF16, name="pair_s%d" % u) for u in range(2)]
+        grouped_w = [keep.tile([P, N, 4], BF16, name="grouped_w%d" % i, align_bytes=64) for i in range(2)]
+        grouped_s = keep.tile([P, S, 4], BF16, name="grouped_s", align_bytes=64)
+        grouped_x = keep.tile([P, S, 4], BF16, name="grouped_x", align_bytes=64)
+        codes_w = [keep.tile([P, N], U32, name="codes_w%d" % i, align_bytes=64) for i in range(2)]
+        scales_w = [keep.tile([P, N], U8, name="scales_w%d" % i, align_bytes=64) for i in range(2)]
+        codes_s = keep.tile([P, S], U32, name="codes_s", align_bytes=64)
+        scales_s = keep.tile([P, S], U8, name="scales_s", align_bytes=64)
+        codes_x = keep.tile([P, S], U32, name="codes_x", align_bytes=64)
+        scales_x = keep.tile([P, S], U8, name="scales_x", align_bytes=64)
+        result = keep.tile([P, M_TILES, S], F32, name="result")
+        acc = [
+            [psum.tile([P, c1 - c0], F32, name="acc%d_%d" % (m, g)) for g, (c0, c1) in enumerate(GROUPS)]
+            for m in range(M_TILES)
+        ]
+
+        w_rows = [w.rearrange("(p j) m -> p j m", j=4) for w in (w1, w2)]
+        s_rows = sT.rearrange("(p u e) t -> p u e t", u=2, e=2)
+        x_rows = xT.rearrange("(p j) n -> p j n", j=4)
+
+        nc.vector.memset(warm[:], 0.0)
+        nc.scalar.activation(out=warm[:], in_=warm[:], func=GELU)
+
+        nc.sync.dma_start(raw_w[1][:], w_rows[1])
+        nc.sync.dma_start(offsets[:], offs)
+        nc.sync.dma_start(raw_s[0][:], s_rows[:, 0])
+        nc.sync.dma_start(raw_s[1][:], s_rows[:, 1])
+        nc.sync.dma_start(raw_w[0][:], w_rows[0])
+        nc.sync.dma_start(bias[:], b.rearrange("(t p) o -> p (t o)", p=P))
+        for i, (c0, c1) in enumerate(X_LOADS):
+            nc.sync.dma_start(raw_x[i][:], x_rows[:, :, c0:c1])
+
+        def split_copy(out, in_, cut):
+            if cut > 0:
+                nc.scalar.copy(out=out[:, 0:cut, :], in_=in_[:, 0:cut, :])
+            if cut < out.shape[1]:
+                nc.vector.tensor_copy(out=out[:, cut:, :], in_=in_[:, cut:, :])
+
+        def quantise(codes, scales, grouped):
+            nc.vector.quantize_mx(
+                out=codes.bitcast(FP8X4), scales=scales, in_=grouped.rearrange("p n j -> p (n j)")
+            )
+
+        grouped_words = grouped_s[:].rearrange("p n j -> p (n j)").bitcast(U32).rearrange("p (n u) -> p n u", u=2)
+
+        split_copy(grouped_w[1][:], raw_w[1][:].rearrange("p j m -> p m j"), 96)
+        quantise(codes_w[1][:], scales_w[1][:], grouped_w[1][:])
+        for u in range(2):
+            split_copy(pair_s[u][:], raw_s[u][:].rearrange("p e t -> p t e"), 352)
+            window = pair_s[u][:].rearrange("p t e -> p (t e)").bitcast(U32)
+            nc.vector.tensor_copy(out=grouped_words[:, :, u], in_=window.indirect(offsets[:]))
+        quantise(codes_s[:], scales_s[:], grouped_s[:])
+        split_copy(grouped_w[0][:], raw_w[0][:].rearrange("p j m -> p m j"), N)
+        quantise(codes_w[0][:], scales_w[0][:], grouped_w[0][:])
+
+        def product(m, g, side, codes, scales):
+            c0, c1 = GROUPS[g]
+            cols = slice(m * P, (m + 1) * P)
+            nc.tensor.matmul_mx(
+                out=acc[m][g][:],
+                lhsT=codes_w[side][:, cols].bitcast(FP8X4),
+                lhsT_scale=scales_w[side][:, cols],
+                rhs=codes[:, c0:c1].bitcast(FP8X4),
+                rhs_scale=scales[:, c0:c1],
+                start=(side == 1),
+                stop=(side == 0),
+            )
+
+        for m in range(M_TILES):
+            for g in range(len(GROUPS)):
+                product(m, g, 1, codes_s, scales_s)
+
+        out_rows = out.rearrange("(t p) n -> p t n", p=P)
+
+        split_copy(grouped_x[:, 0:384], raw_x[0][:].rearrange("p j n -> p n j"), 128)
+        quantise(codes_x[:, 0:256], scales_x[:, 0:256], grouped_x[:, 0:256])
+        quantise(codes_x[:, 256:384], scales_x[:, 256:384], grouped_x[:, 256:384])
+        split_copy(grouped_x[:, 384:512], raw_x[1][:].rearrange("p j n -> p n j"), 32)
+        quantise(codes_x[:, 384:512], scales_x[:, 384:512], grouped_x[:, 384:512])
+        for g, (c0, c1) in enumerate(GROUPS):
+            for m in range(M_TILES):
+                product(m, g, 0, codes_x, scales_x)
+            for m in range(M_TILES):
+                nc.scalar.activation(
+                    out=result[:, m, c0:c1], in_=acc[m][g][:], func=GELU, bias=bias[:, m : m + 1]
+                )
+                if g == 2:
+                    nc.sync.dma_start(out_rows[:, m, 384:512], result[:, m, 384:512])
+            if g == 1:
+                nc.sync.dma_start(out_rows[:, :, 0:384], result[:, :, 0:384])

@@ -16,8 +16,7 @@ P = 128
 M_TILES = N // P
 FLOPS = 2 * 2 * K * S * N
 
-X_LOADS = ((0, 384), (384, 512))
-GROUPS = ((0, 256), (256, 384), (384, 512))
+CHUNKS = ((0, 256), (256, 384), (384, 512))
 
 
 def tile_picked_recall_gelu_e_kernel(tc, xT, sT, w1, w2, b, offs, out):
@@ -31,7 +30,7 @@ def tile_picked_recall_gelu_e_kernel(tc, xT, sT, w1, w2, b, offs, out):
         warm = keep.tile([P, 1], F32, name="warm")
         raw_w = [keep.tile([P, 4, N], F32, name="raw_w%d" % i) for i in range(2)]
         raw_s = [keep.tile([P, 2, T], F32, name="raw_s%d" % u) for u in range(2)]
-        raw_x = [keep.tile([P, 4, c1 - c0], F32, name="raw_x%d" % i) for i, (c0, c1) in enumerate(X_LOADS)]
+        raw_x = [keep.tile([P, 4, c1 - c0], F32, name="raw_x%d" % i) for i, (c0, c1) in enumerate(CHUNKS)]
         pair_s = [keep.tile([P, T, 2], BF16, name="pair_s%d" % u) for u in range(2)]
         grouped_w = [keep.tile([P, N, 4], BF16, name="grouped_w%d" % i, align_bytes=64) for i in range(2)]
         grouped_s = keep.tile([P, S, 4], BF16, name="grouped_s", align_bytes=64)
@@ -44,7 +43,7 @@ def tile_picked_recall_gelu_e_kernel(tc, xT, sT, w1, w2, b, offs, out):
         scales_x = keep.tile([P, S], U8, name="scales_x", align_bytes=64)
         result = keep.tile([P, M_TILES, S], F32, name="result")
         acc = [
-            [psum.tile([P, c1 - c0], F32, name="acc%d_%d" % (m, g)) for g, (c0, c1) in enumerate(GROUPS)]
+            [psum.tile([P, c1 - c0], F32, name="acc%d_%d" % (m, g)) for g, (c0, c1) in enumerate(CHUNKS)]
             for m in range(M_TILES)
         ]
 
@@ -55,20 +54,24 @@ def tile_picked_recall_gelu_e_kernel(tc, xT, sT, w1, w2, b, offs, out):
         nc.vector.memset(warm[:], 0.0)
         nc.scalar.activation(out=warm[:], in_=warm[:], func=GELU)
 
-        nc.sync.dma_start(raw_w[1][:], w_rows[1])
-        nc.sync.dma_start(offsets[:], offs)
         nc.sync.dma_start(raw_s[0][:], s_rows[:, 0])
+        nc.sync.dma_start(offsets[:], offs)
         nc.sync.dma_start(raw_s[1][:], s_rows[:, 1])
+        nc.sync.dma_start(raw_w[1][:], w_rows[1])
         nc.sync.dma_start(raw_w[0][:], w_rows[0])
         nc.sync.dma_start(bias[:], b.rearrange("(t p) o -> p (t o)", p=P))
-        for i, (c0, c1) in enumerate(X_LOADS):
-            nc.sync.dma_start(raw_x[i][:], x_rows[:, :, c0:c1])
+        nc.sync.dma_start(raw_x[0][:], x_rows[:, :, 0:256])
+        nc.sync.dma_start(raw_x[1][:], x_rows[:, :, 256:384])
+        nc.sync.dma_start(raw_x[2][:], x_rows[:, :, 384:512])
 
         def split_copy(out, in_, cut):
             if cut > 0:
                 nc.scalar.copy(out=out[:, 0:cut, :], in_=in_[:, 0:cut, :])
             if cut < out.shape[1]:
                 nc.vector.tensor_copy(out=out[:, cut:, :], in_=in_[:, cut:, :])
+
+        def split_copy4(out, in_, cut):
+            split_copy(out, in_.rearrange("p j n -> p n j"), cut)
 
         def quantise(codes, scales, grouped):
             nc.vector.quantize_mx(
@@ -77,18 +80,12 @@ def tile_picked_recall_gelu_e_kernel(tc, xT, sT, w1, w2, b, offs, out):
 
         grouped_words = grouped_s[:].rearrange("p n j -> p (n j)").bitcast(U32).rearrange("p (n u) -> p n u", u=2)
 
-        split_copy(grouped_w[1][:], raw_w[1][:].rearrange("p j m -> p m j"), 96)
-        quantise(codes_w[1][:], scales_w[1][:], grouped_w[1][:])
-        for u in range(2):
-            split_copy(pair_s[u][:], raw_s[u][:].rearrange("p e t -> p t e"), 352)
-            window = pair_s[u][:].rearrange("p t e -> p (t e)").bitcast(U32)
-            nc.vector.tensor_copy(out=grouped_words[:, :, u], in_=window.indirect(offsets[:]))
-        quantise(codes_s[:], scales_s[:], grouped_s[:])
-        split_copy(grouped_w[0][:], raw_w[0][:].rearrange("p j m -> p m j"), N)
-        quantise(codes_w[0][:], scales_w[0][:], grouped_w[0][:])
+        def prepare_w(i, cut):
+            split_copy4(grouped_w[i][:], raw_w[i][:], cut)
+            quantise(codes_w[i][:], scales_w[i][:], grouped_w[i][:])
 
         def product(m, g, side, codes, scales):
-            c0, c1 = GROUPS[g]
+            c0, c1 = CHUNKS[g]
             cols = slice(m * P, (m + 1) * P)
             nc.tensor.matmul_mx(
                 out=acc[m][g][:],
@@ -100,25 +97,29 @@ def tile_picked_recall_gelu_e_kernel(tc, xT, sT, w1, w2, b, offs, out):
                 stop=(side == 0),
             )
 
-        for m in range(M_TILES):
-            for g in range(len(GROUPS)):
-                product(m, g, 1, codes_s, scales_s)
-
         out_rows = out.rearrange("(t p) n -> p t n", p=P)
 
-        split_copy(grouped_x[:, 0:384], raw_x[0][:].rearrange("p j n -> p n j"), 128)
-        quantise(codes_x[:, 0:256], scales_x[:, 0:256], grouped_x[:, 0:256])
-        quantise(codes_x[:, 256:384], scales_x[:, 256:384], grouped_x[:, 256:384])
-        split_copy(grouped_x[:, 384:512], raw_x[1][:].rearrange("p j n -> p n j"), 32)
-        quantise(codes_x[:, 384:512], scales_x[:, 384:512], grouped_x[:, 384:512])
-        for g, (c0, c1) in enumerate(GROUPS):
+        for u, cut in enumerate((384, 352)):
+            split_copy(pair_s[u][:], raw_s[u][:].rearrange("p e t -> p t e"), cut)
+            window = pair_s[u][:].rearrange("p t e -> p (t e)").bitcast(U32)
+            nc.vector.tensor_copy(out=grouped_words[:, :, u], in_=window.indirect(offsets[:]))
+        prepare_w(1, 256)
+        quantise(codes_s[:], scales_s[:], grouped_s[:])
+        prepare_w(0, 256)
+        for m in range(M_TILES):
+            for g in range(len(CHUNKS)):
+                product(m, g, 1, codes_s, scales_s)
+        for g, cut in enumerate((96, 64, 32)):
+            c0, c1 = CHUNKS[g]
+            split_copy4(grouped_x[:, c0:c1], raw_x[g][:], cut)
+            quantise(codes_x[:, c0:c1], scales_x[:, c0:c1], grouped_x[:, c0:c1])
             for m in range(M_TILES):
                 product(m, g, 0, codes_x, scales_x)
             for m in range(M_TILES):
                 nc.scalar.activation(
                     out=result[:, m, c0:c1], in_=acc[m][g][:], func=GELU, bias=bias[:, m : m + 1]
                 )
-                if g == 2:
-                    nc.sync.dma_start(out_rows[:, m, 384:512], result[:, m, 384:512])
-            if g == 1:
-                nc.sync.dma_start(out_rows[:, :, 0:384], result[:, :, 0:384])
+                if g == len(CHUNKS) - 1:
+                    nc.sync.dma_start(out_rows[:, m, c0:c1], result[:, m, c0:c1])
+            if g < len(CHUNKS) - 1:
+                nc.sync.dma_start(out_rows[:, :, c0:c1], result[:, :, c0:c1])

@@ -1,6 +1,7 @@
 from contextlib import ExitStack
 
 import concourse.mybir as mybir
+from concourse.masks import make_identity
 
 K, T, S, N = 512, 1024, 512, 256
 
@@ -54,15 +55,24 @@ def tile_picked_recall_gelu_e_kernel(tc, xT, sT, w1, w2, b, offs, out):
         nc.vector.memset(warm[:], 0.0)
         nc.scalar.activation(out=warm[:], in_=warm[:], func=GELU)
 
+        ident = keep.tile([P, P], F32, name="ident")
+        bias_rows = keep.tile([P, P], F32, name="bias_rows")
+        bias_turned = psum.tile([P, P], F32, name="bias_turned")
+        nc.gpsimd.memset(bias_rows[:], 0.0)
+        make_identity(nc, ident[:])
+
         nc.sync.dma_start(raw_s[0][:], s_rows[:, 0])
         nc.sync.dma_start(offsets[:], offs)
+        nc.sync.dma_start(bias_rows[0:M_TILES, :], b.rearrange("(t p) o -> t (p o)", p=P))
         nc.sync.dma_start(raw_s[1][:], s_rows[:, 1])
         nc.sync.dma_start(raw_w[1][:], w_rows[1])
         nc.sync.dma_start(raw_w[0][:], w_rows[0])
-        nc.sync.dma_start(bias[:], b.rearrange("(t p) o -> p (t o)", p=P))
         nc.sync.dma_start(raw_x[0][:], x_rows[:, :, 0:256])
         nc.sync.dma_start(raw_x[1][:], x_rows[:, :, 256:384])
         nc.sync.dma_start(raw_x[2][:], x_rows[:, :, 384:512])
+
+        nc.tensor.transpose(bias_turned[:], bias_rows[:], ident[:])
+        nc.vector.tensor_copy(out=bias[:], in_=bias_turned[:, 0:M_TILES])
 
         def split_copy(out, in_, cut):
             if cut > 0:
@@ -71,7 +81,13 @@ def tile_picked_recall_gelu_e_kernel(tc, xT, sT, w1, w2, b, offs, out):
                 nc.vector.tensor_copy(out=out[:, cut:, :], in_=in_[:, cut:, :])
 
         def split_copy4(out, in_, cut):
-            split_copy(out, in_.rearrange("p j n -> p n j"), cut)
+            width = out.shape[1]
+            for engine_copy, a, z in ((nc.scalar.copy, 0, cut), (nc.vector.tensor_copy, cut, width)):
+                if a < z:
+                    engine_copy(
+                        out=out[:, a:z, :].rearrange("p (c i) j -> p c j i", i=4),
+                        in_=in_[:, :, a:z].rearrange("p j (c i) -> p c j i", i=4),
+                    )
 
         def quantise(codes, scales, grouped):
             nc.vector.quantize_mx(
@@ -99,17 +115,44 @@ def tile_picked_recall_gelu_e_kernel(tc, xT, sT, w1, w2, b, offs, out):
 
         out_rows = out.rearrange("(t p) n -> p t n", p=P)
 
-        for u, cut in enumerate((384, 352)):
+        def cast_s(u, cut):
             split_copy(pair_s[u][:], raw_s[u][:].rearrange("p e t -> p t e"), cut)
+
+        def gather(u, c0, c1):
             window = pair_s[u][:].rearrange("p t e -> p (t e)").bitcast(U32)
-            nc.vector.tensor_copy(out=grouped_words[:, :, u], in_=window.indirect(offsets[:]))
-        prepare_w(1, 256)
-        quantise(codes_s[:], scales_s[:], grouped_s[:])
-        prepare_w(0, 256)
+            nc.vector.tensor_copy(
+                out=grouped_words[:, c0:c1, u], in_=window.indirect(offsets[:, c0 // 16 : c1 // 16])
+            )
+
+        def cast_w(i, m, cut):
+            cols = slice(m * P, (m + 1) * P)
+            split_copy4(grouped_w[i][:, cols], raw_w[i][:, :, cols], cut)
+
+        def quantise_w(i, m0, m1):
+            cols = slice(m0 * P, m1 * P)
+            quantise(codes_w[i][:, cols], scales_w[i][:, cols], grouped_w[i][:, cols])
+
+        def quantise_s(c0, c1):
+            quantise(codes_s[:, c0:c1], scales_s[:, c0:c1], grouped_s[:, c0:c1])
+
+        cast_s(0, 288)
+        gather(0, 0, S)
+        cast_s(1, 480)
+        gather(1, 0, 256)
+        cast_w(1, 0, 128)
+        cast_w(1, 1, 128)
+        quantise_w(1, 0, 1)
+        quantise_s(0, 256)
+        gather(1, 256, 512)
+        quantise_w(1, 1, 2)
+        quantise_s(256, 512)
         for m in range(M_TILES):
-            for g in range(len(CHUNKS)):
+            cast_w(0, m, 128)
+        quantise_w(0, 0, 2)
+        for g in range(len(CHUNKS)):
+            for m in range(M_TILES):
                 product(m, g, 1, codes_s, scales_s)
-        for g, cut in enumerate((96, 64, 32)):
+        for g, cut in enumerate((144, 112, 16)):
             c0, c1 = CHUNKS[g]
             split_copy4(grouped_x[:, c0:c1], raw_x[g][:], cut)
             quantise(codes_x[:, c0:c1], scales_x[:, c0:c1], grouped_x[:, c0:c1])

@@ -135,12 +135,20 @@ def tile_picked_recall_gelu_e_kernel(tc, xT, sT, w1, w2, b, offs, out):
         def quantise_s(c0, c1):
             quantise(codes_s[:, c0:c1], scales_s[:, c0:c1], grouped_s[:, c0:c1])
 
-        cast_s(0, 288)
+        cast_s(0, 352)
         gather(0, 0, S)
-        cast_s(1, 480)
+        cast_s(1, 512)
         gather(1, 0, 256)
         cast_w(1, 0, 128)
-        cast_w(1, 1, 128)
+        cols = slice(P, 2 * P)
+        nc.gpsimd.tensor_scalar(
+            out=grouped_w[1][:, cols].rearrange("p (c i) j -> p c j i", i=4),
+            in0=raw_w[1][:, :, cols].rearrange("p j (c i) -> p c j i", i=4),
+            scalar1=1.0,
+            scalar2=0.0,
+            op0=mybir.AluOpType.mult,
+            op1=mybir.AluOpType.add,
+        )
         quantise_w(1, 0, 1)
         quantise_s(0, 256)
         gather(1, 256, 512)
@@ -152,7 +160,7 @@ def tile_picked_recall_gelu_e_kernel(tc, xT, sT, w1, w2, b, offs, out):
         for g in range(len(CHUNKS)):
             for m in range(M_TILES):
                 product(m, g, 1, codes_s, scales_s)
-        for g, cut in enumerate((144, 112, 16)):
+        for g, cut in enumerate((160, 112, 16)):
             c0, c1 = CHUNKS[g]
             split_copy4(grouped_x[:, c0:c1], raw_x[g][:], cut)
             quantise(codes_x[:, c0:c1], scales_x[:, c0:c1], grouped_x[:, c0:c1])

from contextlib import ExitStack

import concourse.mybir as mybir
from concourse.masks import make_identity

K, T, S, N = 512, 1024, 512, 256

F32 = mybir.dt.float32
BF16 = mybir.dt.bfloat16
U32 = mybir.dt.uint32
U16 = mybir.dt.uint16
U8 = mybir.dt.uint8
FP8X4 = mybir.dt.float8_e4m3fn_x4
GELU = mybir.ActivationFunctionType.Gelu_apprx_tanh

P = 128
M_TILES = N // P
FLOPS = 2 * 2 * K * S * N

CHUNKS = ((0, 256), (256, 384), (384, 512))


def tile_picked_recall_gelu_e_kernel(tc, xT, sT, w1, w2, b, offs, out):
    nc = tc.nc
    with ExitStack() as ctx:
        keep = ctx.enter_context(tc.tile_pool(name="keep", bufs=1))
        psum = ctx.enter_context(tc.psum_pool(name="psum", bufs=1))

        offsets = keep.tile([P, S // 16], U16, name="offsets")
        bias = keep.tile([P, M_TILES], F32, name="bias")
        warm = keep.tile([P, 1], F32, name="warm")
        raw_w = [keep.tile([P, 4, N], F32, name="raw_w%d" % i) for i in range(2)]
        raw_s = [keep.tile([P, 2, T], F32, name="raw_s%d" % u) for u in range(2)]
        raw_x = [keep.tile([P, 4, c1 - c0], F32, name="raw_x%d" % i) for i, (c0, c1) in enumerate(CHUNKS)]
        pair_s = [keep.tile([P, T, 2], BF16, name="pair_s%d" % u) for u in range(2)]
        grouped_w = [keep.tile([P, N, 4], BF16, name="grouped_w%d" % i, align_bytes=64) for i in range(2)]
        grouped_s = keep.tile([P, S, 4], BF16, name="grouped_s", align_bytes=64)
        grouped_x = keep.tile([P, S, 4], BF16, name="grouped_x", align_bytes=64)
        codes_w = [keep.tile([P, N], U32, name="codes_w%d" % i, align_bytes=64) for i in range(2)]
        scales_w = [keep.tile([P, N], U8, name="scales_w%d" % i, align_bytes=64) for i in range(2)]
        codes_s = keep.tile([P, S], U32, name="codes_s", align_bytes=64)
        scales_s = keep.tile([P, S], U8, name="scales_s", align_bytes=64)
        codes_x = keep.tile([P, S], U32, name="codes_x", align_bytes=64)
        scales_x = keep.tile([P, S], U8, name="scales_x", align_bytes=64)
        result = keep.tile([P, M_TILES, S], F32, name="result")
        acc = [
            [psum.tile([P, c1 - c0], F32, name="acc%d_%d" % (m, g)) for g, (c0, c1) in enumerate(CHUNKS)]
            for m in range(M_TILES)
        ]

        w_rows = [w.rearrange("(p j) m -> p j m", j=4) for w in (w1, w2)]
        s_rows = sT.rearrange("(p u e) t -> p u e t", u=2, e=2)
        x_rows = xT.rearrange("(p j) n -> p j n", j=4)

        nc.vector.memset(warm[:], 0.0)
        nc.scalar.activation(out=warm[:], in_=warm[:], func=GELU)

        ident = keep.tile([P, P], F32, name="ident")
        bias_rows = keep.tile([P, P], F32, name="bias_rows")
        bias_turned = psum.tile([P, P], F32, name="bias_turned")
        nc.gpsimd.memset(bias_rows[:], 0.0)
        make_identity(nc, ident[:])

        nc.sync.dma_start(raw_s[0][:], s_rows[:, 0])
        nc.sync.dma_start(offsets[:], offs)
        nc.sync.dma_start(bias_rows[0:M_TILES, :], b.rearrange("(t p) o -> t (p o)", p=P))
        nc.sync.dma_start(raw_s[1][:], s_rows[:, 1])
        nc.sync.dma_start(raw_w[1][:], w_rows[1])
        nc.sync.dma_start(raw_w[0][:], w_rows[0])
        nc.sync.dma_start(raw_x[0][:], x_rows[:, :, 0:256])
        nc.sync.dma_start(raw_x[1][:], x_rows[:, :, 256:384])
        nc.sync.dma_start(raw_x[2][:], x_rows[:, :, 384:512])

        nc.tensor.transpose(bias_turned[:], bias_rows[:], ident[:])
        nc.vector.tensor_copy(out=bias[:], in_=bias_turned[:, 0:M_TILES])

        def split_copy(out, in_, cut):
            if cut > 0:
                nc.scalar.copy(out=out[:, 0:cut, :], in_=in_[:, 0:cut, :])
            if cut < out.shape[1]:
                nc.vector.tensor_copy(out=out[:, cut:, :], in_=in_[:, cut:, :])

        def split_copy4(out, in_, cut):
            width = out.shape[1]
            for engine_copy, a, z in ((nc.scalar.copy, 0, cut), (nc.vector.tensor_copy, cut, width)):
                if a < z:
                    engine_copy(
                        out=out[:, a:z, :].rearrange("p (c i) j -> p c j i", i=4),
                        in_=in_[:, :, a:z].rearrange("p j (c i) -> p c j i", i=4),
                    )

        def quantise(codes, scales, grouped):
            nc.vector.quantize_mx(
                out=codes.bitcast(FP8X4), scales=scales, in_=grouped.rearrange("p n j -> p (n j)")
            )

        grouped_words = grouped_s[:].rearrange("p n j -> p (n j)").bitcast(U32).rearrange("p (n u) -> p n u", u=2)

        def prepare_w(i, cut):
            split_copy4(grouped_w[i][:], raw_w[i][:], cut)
            quantise(codes_w[i][:], scales_w[i][:], grouped_w[i][:])

        def product(m, g, side, codes, scales):
            c0, c1 = CHUNKS[g]
            cols = slice(m * P, (m + 1) * P)
            nc.tensor.matmul_mx(
                out=acc[m][g][:],
                lhsT=codes_w[side][:, cols].bitcast(FP8X4),
                lhsT_scale=scales_w[side][:, cols],
                rhs=codes[:, c0:c1].bitcast(FP8X4),
                rhs_scale=scales[:, c0:c1],
                start=(side == 1),
                stop=(side == 0),
            )

        out_rows = out.rearrange("(t p) n -> p t n", p=P)

        def cast_s(u, cut):
            split_copy(pair_s[u][:], raw_s[u][:].rearrange("p e t -> p t e"), cut)

        def gather(u, c0, c1):
            window = pair_s[u][:].rearrange("p t e -> p (t e)").bitcast(U32)
            nc.vector.tensor_copy(
                out=grouped_words[:, c0:c1, u], in_=window.indirect(offsets[:, c0 // 16 : c1 // 16])
            )

        def cast_w(i, m, cut):
            cols = slice(m * P, (m + 1) * P)
            split_copy4(grouped_w[i][:, cols], raw_w[i][:, :, cols], cut)

        def quantise_w(i, m0, m1):
            cols = slice(m0 * P, m1 * P)
            quantise(codes_w[i][:, cols], scales_w[i][:, cols], grouped_w[i][:, cols])

        def quantise_s(c0, c1):
            quantise(codes_s[:, c0:c1], scales_s[:, c0:c1], grouped_s[:, c0:c1])

        cast_s(0, 352)
        gather(0, 0, S)
        cast_s(1, 512)
        gather(1, 0, 256)
        cast_w(1, 0, 128)
        cols = slice(P, 2 * P)
        nc.gpsimd.tensor_scalar(
            out=grouped_w[1][:, cols].rearrange("p (c i) j -> p c j i", i=4),
            in0=raw_w[1][:, :, cols].rearrange("p j (c i) -> p c j i", i=4),
            scalar1=1.0,
            scalar2=0.0,
            op0=mybir.AluOpType.mult,
            op1=mybir.AluOpType.add,
        )
        quantise_w(1, 0, 1)
        quantise_s(0, 256)
        gather(1, 256, 512)
        quantise_w(1, 1, 2)
        quantise_s(256, 512)
        for m in range(M_TILES):
            cast_w(0, m, 128)
        quantise_w(0, 0, 2)
        for g in range(len(CHUNKS)):
            for m in range(M_TILES):
                product(m, g, 1, codes_s, scales_s)
        for g, cut in enumerate((160, 112, 16)):
            c0, c1 = CHUNKS[g]
            split_copy4(grouped_x[:, c0:c1], raw_x[g][:], cut)
            quantise(codes_x[:, c0:c1], scales_x[:, c0:c1], grouped_x[:, c0:c1])
            for m in range(M_TILES):
                product(m, g, 0, codes_x, scales_x)
            for m in range(M_TILES):
                nc.scalar.activation(
                    out=result[:, m, c0:c1], in_=acc[m][g][:], func=GELU, bias=bias[:, m : m + 1]
                )
                if g == len(CHUNKS) - 1:
                    nc.sync.dma_start(out_rows[:, m, c0:c1], result[:, m, c0:c1])
            if g < len(CHUNKS) - 1:
                nc.sync.dma_start(out_rows[:, :, c0:c1], result[:, :, c0:c1])
